import numpy as np, ml_dtypes
CORES = [23,119,17,113]
N = 4
BF = ml_dtypes.bfloat16
def gentries(a):
    return np.ascontiguousarray(a.reshape(8, 16, -1).transpose(0, 2, 1)).reshape(8, -1)
def gtable(e):
    e = np.asarray(e); return np.ascontiguousarray(e.reshape(8, -1, 16).transpose(0, 2, 1)).reshape(128, -1).astype(np.int32)
V, B, CAP, D, VOTE, RO, ST = 1024, 256, 64, 4, 9, 3, 1024
def ranks():
    return np.arange(N).reshape(N, 1, 1, 1)
def heights(rng):
    b = rng.integers(0, 256, (N, 8, 1, V)); b[..., :B] += rng.choice(np.array([-30, 0, 40, 90]), (N, 8, 1, 1))
    return np.clip(b + rng.integers(-60, 61, (N, 8, 16, V)), 0, 255)
def weights(rng):
    return np.clip(rng.integers(0, 256, (N, 8, 1, D, V)) + rng.integers(-60, 61, (N, 8, 16, D, V)), 0, 255)
def names(rng):
    s = (N, 8, D, V); r = ranks()
    own = np.where(rng.random(s) < 0.5, (np.arange(V) + rng.integers(-24, 25, s)) % V, rng.integers(0, V, s))
    return np.where(rng.random(s) < 0.7, ST * r + own, ST * ((r + rng.integers(1, N, s)) % N) + rng.integers(0, B, s))
def pack(h, w, n):
    return {"h0": h.reshape(N, 128, V).astype(np.float32).astype(BF), "w0": w.reshape(N, 128, D * V).astype(np.float32).astype(BF), "nb": np.stack([gtable(a.reshape(8, -1)) for a in n])}
def setup_inputs(rng):
    h = heights(rng); w = weights(rng); n = names(rng)
    return pack(h, w, n)
def elsewhere(p):
    return np.concatenate([ST * q + np.arange(B) for q in range(N) if q != p])
def setup_inputs_room(rng):
    w = weights(rng); n = names(rng); h = np.zeros((N, 8, 16, V), np.int64); tops = np.zeros((N, 8, V), bool)
    for q in range(N):
        for g in range(8):
            k = int(rng.choice(np.array([0, 1, CAP - 1, CAP, CAP + 1, B])))
            if q < 2: k = (CAP, CAP + 1, B, CAP - 1, 1, 0, CAP, CAP + 1)[(g + 3 * q) % 8]
            top = np.zeros(V, bool); top[rng.permutation(B)[:k]] = True; top[B + rng.permutation(V - B)[:(V - B) // 4]] = True
            inner = B + np.flatnonzero(top[B:]); low = B + np.flatnonzero(~top[B:]); tops[q, g] = top
            h[q, g] = np.where(top, rng.integers(160, 256, (16, V)), rng.integers(0, 120, (16, V)))
            n[q, g] = np.where(top, ST * q + rng.choice(low, (D, V)), n[q, g])
            n[q, g, D - 1] = np.where(top, n[q, g, D - 1], ST * q + rng.choice(inner, V))
    a, b = [int(x) for x in 2 + rng.permutation(N - 2)[:2]]
    dead = np.concatenate([ST * q + np.flatnonzero(tops[q, 0, :B])[:CAP] for q in range(N) if q != a])
    h[a, 0] = rng.integers(0, 120, (16, V)); w[a, 0, :, 0] = rng.integers(200, 256, (16, V))
    n[a, 0, 0] = rng.choice(dead, V)
    n[a, 0, 1:] = rng.permutation(np.resize(elsewhere(a), (D - 1) * V)).reshape(D - 1, V)
    h[b, 1] = np.where(rng.random(V) < 0.5, rng.integers(245, 256, (16, V)), rng.integers(0, 120, (16, V)))
    n[b, 1] = rng.permutation(np.resize(elsewhere(b), D * V)).reshape(D, V)
    low = rng.permutation(B)[CAP:]; top = np.ones(V, bool); top[low] = False
    h[a, 2] = np.where(top, rng.integers(160, 256, (16, V)), rng.integers(0, 120, (16, V)))
    t = ST * a + rng.choice(low, (D, V)); t[:, low] = ST * a + rng.integers(B, V, (D, low.size)); t[0, low] = ST * a + V - 1 - rng.permutation(low.size)
    n[a, 2] = t
    return pack(h, w, n)
def setup_inputs_ties(rng):
    n = names(rng); me = ST * ranks() + np.arange(V)
    c = rng.choice(np.array([0, 0, 0, 0, 0, 0, 0, VOTE - 1, VOTE, VOTE, 16]), (N, 8, 1, V))
    h = rng.integers(20, 200, (1, 8, 1, 1)) + (np.argsort(rng.random((N, 8, 16, V)), axis=2) < c)
    w = rng.choice(np.array([0, 60, 120, 180]), (N, 8, 1, D, V)) + 3 * ((np.arange(16).reshape(16, 1, 1) + rng.integers(0, 16, (N, 8, 1, D, V))) % 16)
    n[:, :, 1] = np.where(rng.random((N, 8, V)) < 0.3, n[:, :, 0], n[:, :, 1])
    n[:, :, D - 1] = np.where(rng.random((N, 8, V)) < 0.2, n[:, :, 0], n[:, :, D - 1])
    n = np.where(rng.random(n.shape) < 0.1, me, n)
    return pack(h, w, n)
def late(rng, h, n, g):
    s = (D, V)
    for q in range(N):
        o = B + rng.permutation(V - B); y, z = int(o[0]), int(o[1]); low = np.concatenate([np.arange(B), o[2:]])
        h[q, g] = rng.integers(0, 120, (16, V)); h[q, g, :, z] = rng.integers(150, 190, 16); h[q, g, :, y] = rng.integers(200, 256, 16)
        t = np.where(rng.random(s) < 0.7, ST * q + rng.choice(low, s), ST * ((q + rng.integers(1, N, s)) % N) + rng.integers(0, B, s))
        l = rng.integers(0, D, V); t[l, np.arange(V)] = ST * q + z; t[l[z], z] = ST * q + y
        n[q, g] = t
def setup_inputs_alike(rng):
    h = heights(rng) // 2; w = weights(rng); n = names(rng); r = ranks(); s = (N, 4, D, V); hub = np.array([0, B - 1, V - 1])
    mine = ST * r + rng.choice(hub, s); far = ST * ((r + rng.integers(1, N, s)) % N) + rng.choice(hub[:2], s)
    n[:, 1::2] = np.where(rng.random(s) < 0.5, mine, far)
    n[:, ::4] = np.array(n[:, ::4, :1])
    h[..., hub] = rng.integers(200, 256, (N, 8, 16, 3)); n[..., hub] = ST * r + rng.integers(B, V - 1, (N, 8, D, 3))
    late(rng, h, n, int(rng.choice(np.array([2, 6]))))
    return pack(h, w, n)
def setup_inputs_bare(rng):
    h = heights(rng); w = weights(rng); n = names(rng); r = ranks(); me = ST * r + np.arange(V); nx = ST * r + (np.arange(V) + 1) % V
    n = np.where(rng.random(n.shape) < 0.4, me, n); g = rng.permutation(8); q = rng.permutation(N)
    h[:, g[0]] = 77; n[:, g[0]] = np.where(n[:, g[0]] == me[:, 0], nx[:, 0], n[:, g[0]])
    n[q[0], g[1]] = me[q[0], 0]
    w[:, g[2]] = 0
    return pack(h, w, n)
def setup_inputs_spread(rng):
    h = (np.exp2(8 * rng.random((N, 8, 1, V))) * rng.random((N, 8, 16, V))).astype(np.int64)
    w = np.minimum((2 * np.exp2(8 * rng.random((N, 8, 1, D, V))) * rng.random((N, 8, 16, D, V))).astype(np.int64), 255)
    s = (N, 8, D, V); r = ranks(); u = rng.random(s) ** 3
    n = np.where(rng.random(s) < 0.6, ST * r + (V * u).astype(np.int64), ST * ((r + rng.integers(1, N, s)) % N) + (B * u).astype(np.int64))
    return pack(h, w, n)
def check_inputs(d):
    bad = []
    for k in ("h0", "w0"):
        a = np.asarray(d[k]).astype(np.float64)
        if not np.all((a >= 0) & (a <= 255) & (a == np.floor(a))): bad.append("whole numbers from 0 to 255 in " + k)
    e = np.stack([gentries(a) for a in d["nb"]]).astype(np.int64); q = e // ST; v = e - ST * q
    if not np.all((q >= 0) & (q < N) & (v < np.where(q == np.arange(N).reshape(N, 1, 1), V, B))): bad.append("names in nb")
    return bad
def reference(h0, w0, nb):
    h = h0.astype(np.float32).astype(np.int32).reshape(N, 8, 16, V); w = w0.astype(np.float32).astype(np.int32).reshape(N, 8, 16, D, V)
    m = np.stack([gentries(a) for a in nb]).astype(np.int64).reshape(N, 8, D, V); m = (m // ST) * V + m % ST
    live = np.ones((N, 8, V), bool); rising = (2 * D - 1 - np.arange(2 * D)).reshape(2 * D, 1)
    for rnd in range(RO):
        hg = h.transpose(1, 2, 0, 3).reshape(8, 16, N * V); wg = w.transpose(1, 2, 3, 0, 4).reshape(8, 16, D, N * V); mg = m.transpose(1, 2, 0, 3).reshape(8, D, N * V)
        die = []
        for r in range(N):
            a = np.take_along_axis(hg, m[r].reshape(8, 1, D * V), 2).reshape(8, 16, D, V)
            votes = np.add.reduce((h[r][:, :, None, :] > a).astype(np.int32), axis=1)
            die.append(np.all((votes >= VOTE) | (m[r] == r * V + np.arange(V)), axis=1))
        die = np.stack(die) & live
        e = die[:, :, :B].astype(np.int64); before = np.add.accumulate(e, axis=2) - e
        die[:, :, :B] = (e == 1) & (before < CAP)
        live = live & ~die; dg = die.transpose(1, 0, 2).reshape(8, N * V)
        hn, wn, mn = [], [], []
        for r in range(N):
            me = r * V + np.arange(V)
            gone = np.take_along_axis(dg, m[r].reshape(8, D * V), 1).reshape(8, D, V)
            hit = live[r] & np.any(gone, axis=1)
            s = np.argmax(gone, axis=1)[:, None, :]; d = np.take_along_axis(m[r], s, 1)
            ws = np.take_along_axis(w[r], s[:, None], 2)
            wd = np.take_along_axis(wg, d[:, None], 3); hd = np.take_along_axis(hg, d, 2)[:, :, None, :]
            cw = np.concatenate([w[r], np.clip(ws + wd - hd, 0, 255)], axis=2)
            cm = np.concatenate([m[r], np.take_along_axis(mg, d, 2)], axis=1)
            q = cm // V; v = cm - q * V
            out = (cm == me) | np.take_along_axis(dg, cm.reshape(8, -1), 1).reshape(cm.shape) | ((q != r) & (v >= B))
            key = np.where(out, -1, 2 * D * np.add.reduce(cw, axis=1) + rising)
            twin = np.any((cm[:, :, None] == cm[:, None]) & (key[:, :, None] > key[:, None]), axis=1)
            key = np.where(twin, -1, key)
            o = np.argsort(-key, axis=1, kind="stable")[:, :D]; full = np.take_along_axis(key, o, 1) >= 0
            nm = np.where(full, np.take_along_axis(cm, o, 1), me); nw = np.where(full[:, None], np.take_along_axis(cw, o[:, None], 2), 0)
            mn.append(np.where(hit[:, None], nm, m[r])); wn.append(np.where(hit[:, None, None], nw, w[r]))
            hn.append(np.where(hit[:, None], (h[r] + np.maximum(h[r], ws[:, :, 0])) >> 1, h[r]))
        h, w, m = np.stack(hn), np.stack(wn), np.stack(mn)
    m = (m // V) * ST + m % V
    return {"yh": h.reshape(N, 128, V).astype(np.float32).astype(BF), "yw": w.reshape(N, 128, D * V).astype(np.float32).astype(BF), "yn": np.stack([gtable(a.reshape(8, -1)) for a in m]).astype(np.float32)}

from concourse.bass import DstId, RemoteDMATransfer
from concourse.mybir import AluOpType as A, AxisListType, ActivationFunctionType as F

V, B, RO, PW = 1024, 256, 3, 1808
RA, Z1, WA, CW, WB_, Z2, RB, WEND = 0, 4096, 4160, 8256, 12352, 16448, 16512, 20608
BIG = float(2 ** 24)
KOA = 12
bf, f32, i32, u16 = "bfloat16", "float32", "int32", "uint16"
SCRATCH = {"HL": ("sbuf", [128, 4, 128], i32), "RI": ("sbuf", [128, 4, 128], i32)}
for _d, _l in ((bf, dict(H=RO * PW, HO=2 * V, TT=RO * PW, M=RO * PW, MX=RO * B, W=WEND, YW=4096, ST=RO * V, CMP=4096, G=4096,
                         WD=4096, MD=V, WS=V, TN=V, HU=V, HF=V, TS=V, CL=1536, EMP=256, DUP=256, GS=256, DEAD=64, DIE=64, HIT=64,
                         FL=256, FM2=128, EB=16, ES=16, ZERO=16, PEN=256, EM=256, E=1024, EE=384, AL=192, GT=384, EG=384,
                         HALF=64, ONE=128, GE=128, GE0=128, GN1=128, UN0=128, UN=128, IM=768, BX=128, XM=2048, DM=1024,
                         FM=7 * 144, KK=1024)),
               (f32, dict(N=256, NZ=256, YN=256, ZA=256, ZB=128, ZC=128, FE=64, FO=256, T2=256, U=256, XX=384, SC=13 * 128,
                          db=256, de=256, KS=256, MK=16, AV=32, PF=2, XI=64, X=64, ME=256, MC=128, ZS=512, UI=256, UH=256, UL=256)),
               (i32, dict(NB=256, t1=256, t2=256, ZI=128, ZD=128, NCI=256, LOC=256, HIC=256, da=256, ia=16, ib=16, PI=2,
                          MI=64, MJ=128)),
               (u16, dict(N16=256, OD=64, OS=64, OW=256, OM=256))):
    for _k in _l:
        SCRATCH[_k] = ("sbuf", [128, _l[_k]], _d)
for _b in range(8):
    SCRATCH["P%d" % _b] = ("psum", [128, 512], f32)
SEMAPHORES = ["cv", "cs", "cp", "cg", "ldn", "ldb", "ldi", "ldo", "ldw0", "ldw1", "ldw2", "out", "hs"]
for _r in range(RO):
    SEMAPHORES += ["%s%d" % (_n, _r) for _n in ("aH", "aT", "aM", "aW", "sH", "sT", "sM", "sW", "cp_", "st")]


def helper_of(core, T, topo):
    free = [c for c in topo.cores_of(core) if T.rank_of(c) is None and topo.die(c) == topo.die(core)]
    return free[0]


def dst(topo, c):
    a = topo.addr(c)
    return DstId(rid=a[0], pnc=a[1])


def bits(engs):
    m = 0
    for e in engs:
        m |= 1 << e
    return m


def helper_program(g, core, T, topo, q):
    src = T.cores[q]
    far = [c for c in T.cores if topo.chip(c) != topo.chip(src)]
    eng = topo.engines(core, far[0])
    n = len(eng) // 4
    for r in range(RO):
        base = (RA if r % 2 == 0 else RB) + B * q
        g.wait_ge(T.sem["st%d" % r], 8)
        g.remote_dma_fused([RemoteDMATransfer(
            dst_ids=[dst(topo, c) for c in far], dma_engine_mask=bits(eng[n * l:n * l + n]), remote_sem=T.sem["aW%d" % r],
            srcs=[T.ST[:, r * V + l * B:r * V + (l + 1) * B]],
            dsts=[T.W[:, base + l * V:base + l * V + B] for c in far]) for l in range(4)], local_sem=T.sem.hs)
    g.wait_ge(T.sem.hs, RO * 4 * n)


def rank_program(g, core, T, topo):
    rank = T.rank_of(core)
    if rank is None:
        for q, c in enumerate(T.cores):
            if helper_of(c, T, topo) == core:
                helper_program(g, core, T, topo, q)
        return
    others = [c for c in T.cores if c != core]
    near = [c for c in others if topo.chip(c) == topo.chip(core)]
    far = [c for c in others if topo.chip(c) != topo.chip(core)]
    efar = topo.engines(core, far[0])
    enear = [e for e in topo.engines(core, near[0]) if e not in efar]
    hlp = helper_of(core, T, topo)
    Q = {"v": g.vector, "s": g.scalar, "p": g.tensor, "g": g, "y": g.sync}
    own = {"v": "cv", "s": "cs", "p": "cp", "g": "cg"}
    cnt = {}
    seen = {e: {} for e in Q}
    lastw, reads, bank = {}, {}, {}
    S = T.sem
    P = [T["P%d" % b] for b in range(8)]

    def wait(e, tok):
        if seen[e].get(tok[0], 0) < tok[1]:
            Q[e].wait_ge(S[tok[0]], tok[1])
            seen[e][tok[0]] = tok[1]

    def pre(e, r, w, bk):
        need = {}
        toks = [lastw[k] for k in r if k in lastw]
        for k in w:
            toks += [t for t in [lastw.get(k)] + reads.get(k, []) if t is not None and t[0] != own.get(e)]
        for b in bk:
            toks += [t for t in bank.get(b, {}).values() if t[0] != own.get(e)]
        for t in toks:
            if not (e == "p" and t[0] == "cp"):
                need[t[0]] = max(need.get(t[0], 0), t[1])
        for k in need:
            wait(e, (k, need[k]))

    def post(e, tok, r, w, bk):
        for k in r:
            reads.setdefault(k, []).append(tok)
        for k in w:
            lastw[k] = tok
            reads[k] = []
        for b in bk:
            bank.setdefault(b, {})[e] = tok

    def op(e, emit, r=(), w=(), bk=(), sem=None, n=1):
        pre(e, r, w, bk)
        ins = emit()
        sem = sem or own[e]
        cnt[sem] = cnt.get(sem, 0) + n
        ins.then_inc(S[sem], n)
        post(e, (sem, cnt[sem]), r, w, bk)

    def tt(o, a, b, alu, r, w, bk=()):
        op("v", lambda: g.vector.tensor_tensor(o, a, b, alu), r, w, bk)

    def ts(o, a, s1, o0, r, w, bk=(), s2=None, o1=None):
        if o1 is None:
            op("v", lambda: g.vector.tensor_scalar(o, a, s1, None, o0), r, w, bk)
        else:
            op("v", lambda: g.vector.tensor_scalar(o, a, s1, s2, o0, o1), r, w, bk)

    def cp(o, a, r, w, bk=()):
        op("v", lambda: g.vector.tensor_copy(o, a), r, w, bk)

    def ms(o, c, w):
        op("v", lambda: g.vector.memset(o, c), (), w)

    def act(o, a, r, w, bk=(), fn=None, scale=1.0, bias=0.0):
        op("s", lambda: g.scalar.activation(o, a, fn or F.Identity, bias, scale), r, w, bk)

    def gather(e, o, x, r, w):
        if e == "v":
            cp(o, x, r, w)
        else:
            act(o, x, r, w)

    def mm(lst, r, w, bk):
        def emit():
            ins = None
            for (o, l, x, st, sp) in lst:
                ins = g.tensor.matmul(o, l, x, st, sp)
            return ins
        op("p", emit, r, w, bk)

    def dma(e, o, a, r, w, sem):
        op(e, lambda: Q[e].dma_start(o, a), r, w, (), sem, 16)

    def send(transfers, r, sem):
        pre("g", r, (), ())
        g.remote_dma_fused(transfers, local_sem=S[sem])
        cnt[sem] = 8
        post("g", (sem, 8), r, (), ())

    def small(ap_src, ap_dst, r, arr, sem):
        send([RemoteDMATransfer(dst_ids=[dst(topo, c) for c in far + near], dma_engine_mask=bits(efar), remote_sem=S[arr],
                                srcs=[ap_src], dsts=[ap_dst for c in others])], r, sem)

    I1, In, Ih, Ihn, Ibig, I16 = [T.IM[:, j * 128:(j + 1) * 128] for j in range(6)]

    def FM(j, i):
        return T.FM[:, j * 144 + 15 - i:j * 144 + 143 - i]

    def XM(i):
        return T.XM[:, i * 128:(i + 1) * 128]

    def DM(i):
        return T.DM[:, i * 128:(i + 1) * 128]

    def l64(t, a, o=0):
        return t[:, o + 64 * a:o + 64 * (a + 1)]
    cb = 16 + B * rank
    ci = 16 + V

    def wsend(r):
        w0 = WA if r % 2 == 0 else WB_
        base = (RA if r % 2 == 0 else RB) + B * rank
        kw = "w%d" % (r % 2)
        if r == 2:
            wait("g", ("aH2", 24))
        n = len(enear) // 4
        send([RemoteDMATransfer(dst_ids=[dst(topo, hlp), dst(topo, near[0])], dma_engine_mask=bits(enear[n * l:n * l + n]),
                                remote_sem=S["st%d" % r], srcs=[T.W[:, w0 + l * V:w0 + l * V + B]],
                                dsts=[T.ST[:, r * V + l * B:r * V + (l + 1) * B], T.W[:, base + l * V:base + l * V + B]])
              for l in range(4)], [kw + "b%d" % l for l in range(4)], "sW%d" % r)
        if r > 0:
            for l in range(4):
                dma("y", T.W[:, base + l * V:base + l * V + B], T.W[:, w0 + l * V:w0 + l * V + B], [kw + "b%d" % l],
                    ["r%do%d" % (r % 2, l)], "cp_%d" % r)
            for l in range(4):
                lastw["r%do%d" % (r % 2, l)] = ("cp_%d" % r, 64)
                reads[kw + "b%d" % l][-1] = ("cp_%d" % r, 64)

    dma("y", T.H[:, cb:cb + B], T.h0[:, 0:B], [], ["h0b"], "ldb")
    dma("s", T.NB[:], T.nb[:], [], ["NB"], "ldn")
    dma("y", T.H[:, ci:ci + V - B], T.h0[:, B:V], [], ["h0i"], "ldi")
    dma("s", T.HO[:, 0:V], T.h0[:], [], ["o0"], "ldo")
    for l in range(4):
        dma("y", T.W[:, WA + l * V:WA + l * V + B], T.w0[:, l * V:l * V + B], [], [], "ldw0")
    for l in range(4):
        dma("y", T.W[:, WA + l * V + B:WA + (l + 1) * V], T.w0[:, l * V + B:(l + 1) * V], [], [], "ldw1")
    for l in range(4):
        dma("y", T.W[:, RA + B * rank + l * V:RA + B * rank + l * V + B], T.w0[:, l * V:l * V + B], [], [], "ldw2")
    for l in range(4):
        lastw["w0b%d" % l] = ("ldw0", 64)
        lastw["w0i%d" % l] = ("ldw1", 64)
        lastw["r0o%d" % l] = ("ldw2", 64)
    lastw["o0a"] = lastw["o0b"] = lastw["o0"]

    def gp(emit, r, w):
        op("g", emit, r, w)
    ms(T.ONE[:], 1.0, ["ONE"])
    ms(T.FM[:], 0.0, ["FM"])
    gp(lambda: g.iota(T.ia[:], [[-1, 16]], 16, 1), [], ["ia"])
    gp(lambda: g.iota(T.XI[:], [[16, 64]], 0, 0, allow_small_or_imprecise_dtypes=True), [], ["XI"])
    gp(lambda: g.iota(T.PI[:, 0:1], [[0, 1]], 0, 1), [], ["PI"])
    gp(lambda: g.affine_select(I1, T.ONE[:], [[-1, 128]], A.is_equal, 0.0, 0, 1), ["ONE"], ["I1"])
    gp(lambda: g.affine_select(T.GE0[:], T.ONE[:], [[-16, 8], [0, 16]], A.is_ge, 0.0, 0, 1), ["ONE"], ["GE0"])
    gp(lambda: g.affine_select(T.GE[:], T.GE0[:], [[16, 8], [0, 16]], A.is_gt, 0.0, 16, -1), ["GE0"], ["GE"])
    small(T.H[:, cb:cb + B], T.H[:, cb:cb + B], ["h0b"], "aH0", "sH0")
    gp(lambda: g.iota(T.UI[:], [[1, 256]], 16, 0, allow_small_or_imprecise_dtypes=True), [], ["UI"])
    for k in range(RO):
        ms(T.H[:, k * PW:k * PW + 16], 0.0, ["pad"])
        ms(T.TT[:, k * PW:k * PW + 16], 0.0, ["pad"])
        ms(T.M[:, k * PW:k * PW + 16], -64.0, ["pad"])
    ms(T.W[:, Z1:WA], 0.0, ["pad"])
    ms(T.W[:, Z2:RB], 0.0, ["pad"])
    ms(T.ZERO[:], 0.0, ["ZERO"])
    ms(T.DEAD[:], 0.0, ["DEAD"])
    ms(T.BX[:], 0.0, ["BX"])
    ms(T.HALF[:], 0.5, ["HALF"])
    ts(T.ib[:], T.ia[:], 15, A.bitwise_and, ["ia"], ["ib"])
    ts(T.PI[:, 1:2], T.PI[:, 0:1], 15, A.bitwise_and, ["PI"], ["PI1"])
    ts(T.MK[:], T.ib[:], 0.0, A.is_equal, ["ib"], ["MK"])
    cp(T.PF[:, 0:1], T.PI[:, 1:2], ["PI1"], ["PF"])
    ts(T.X[:], T.XI[:], T.PF[:, 0:1], A.add, ["XI", "PF"], ["X"])
    NP = P[1][:, 256:512]
    ts(T.t1[:], T.NB[:], 2, A.arith_shift_right, ["NB"], ["t1"], (), 768, A.bitwise_and)
    ts(T.t2[:], T.NB[:], 1023, A.bitwise_and, ["NB"], ["t2"])
    ts(P[1][:, 0:256], T.t2[:], 256.0, A.is_ge, ["t2"], ["t3"], [1], 768.0, A.mult)
    tt(P[1][:, 0:256], P[1][:, 0:256], T.t1[:], A.max, ["t1", "t3"], ["t3"], [1])
    tt(P[1][:, 0:256], P[1][:, 0:256], T.t2[:], A.add, ["t3", "t2"], ["t3"], [1])
    ts(T.N16[:], P[1][:, 0:256], 16.0, A.add, ["t3"], ["N16"], [1])
    ts(NP, P[1][:, 0:256], 16.0, A.add, ["t3"], ["NP"], [1])
    red = lambda o, a: op("v", lambda: g.vector.tensor_reduce(o, a, AxisListType.X, A.add), ["MK"], ["AVa"])
    for j in range(3):
        red(T.AV[:, 12 + j:13 + j], T.MK[:, j:16:4])
    ts(T.AV[:, 28:29], T.AV[:, 14:15], -64.0, A.mult, ["AVa"], ["AVd"])
    ts(T.AV[:, 16:17], T.AV[:, 13:14], float(rank), A.mult, ["AVa"], ["AVf"])
    for k in range(1, 4):
        ts(T.AV[:, 16 + k:17 + k], T.AV[:, 13:14], float(3 + k), A.mult, ["AVa", "AVd"], ["AVf"], (), T.AV[:, 28:29], A.add)
    for l in range(4):
        act(T.ME[:, 64 * l:64 * l + 16], T.X[:, 0:16], ["X"], ["ME"], bias=float(cb))
        act(T.ME[:, 64 * l + 16:64 * l + 64], T.X[:, 16:64], ["X"], ["ME"], bias=float(ci - B))
    act(I16, I1, ["I1"], ["I16"], scale=16.0)
    act(Ibig, I1, ["I1"], ["Ibig"], scale=-BIG)
    act(T.GN1[:], T.GE[:], ["GE"], ["GN1"], scale=-1.0)
    act(T.FM[:, 15:143:16], T.GE[:, 0:128:16], ["GE", "FM"], ["F0"])
    act(In, I1, ["I1"], ["In"], scale=-1.0)
    gp(lambda: g.affine_select(T.UN0[:], T.GN1[:], [[-1, 128]], A.is_gt, 0.0, 0, 1), ["GN1"], ["UN0"])
    gp(lambda: g.affine_select(T.UN[:], T.UN0[:], [[-1, 128]], A.not_equal, -128.0, 0, 1), ["UN0"], ["UN"])
    wsend(0)
    act(T.BX[:, 1:128:4], T.GE[:, 1:128:4], ["GE", "BX"], ["BX1"], scale=-64.0)
    act(T.BX[:, 3:128:4], T.GE[:, 3:128:4], ["GE", "BX"], ["BX3"])
    for i in range(16):
        act(XM(i), T.BX[:], ["BX1", "BX3", "MK"], ["XM"], scale=T.MK[:, i:i + 1])
    ts(P[2][:, 0:256], T.UI[:], 256.0, A.is_ge, ["UI", "AVa"], ["UH"], [2], T.AV[:, 13:14], A.mult)
    ts(T.UL[:, 0:240], T.UI[:, 0:240], T.AV[:, 12:13], A.mult, ["UI", "AVa"], ["UL"])
    ts(T.UL[:, 240:256], T.UI[:, 240:256], -256.0, A.add, ["UI", "AVa"], ["UL"], (), T.AV[:, 12:13], A.mult)
    tt(T.EMP[:], NP, T.ME[:], A.is_equal, ["NP", "ME"], ["EMP"], [1])
    tt(T.UH[:], P[2][:, 0:256], T.UL[:], A.add, ["UH", "UL"], ["UH"], [2])
    for k in range(4):
        act(T.TS[:, k * B:(k + 1) * B], T.UH[:], ["UH", "AVf"], ["TS"], bias=T.AV[:, 16 + k:17 + k])
    for l in range(4):
        red(T.AV[:, l:l + 1], T.MK[:, 4 * l:4 * l + 2])
        red(T.AV[:, 4 + l:5 + l], T.MK[:, 4 * l:4 * l + 3])
    ts(T.AV[:, 20:24], T.MK[:, 0:16:4], -255.0, A.mult, ["MK"], ["AVb"])
    ts(T.AV[:, 24:28], T.AV[:, 4:8], 256.0, A.mult, ["AVa"], ["AVc"])
    tt(T.AV[:, 8:12], T.AV[:, 20:24], T.AV[:, 24:28], A.add, ["AVb", "AVc"], ["AVe"])

    def nz():
        for l in range(4):
            act(l64(T.NZ, l), l64(P[1], l, 256), ["NP"], ["NZ"], [1], bias=float(2048 * (4 - l)))
        act(T.N[:], NP, ["NP"], ["N"], [1])

    def late_scalar():
        act(T.FM[:, 2 * 144 + 15:2 * 144 + 143:16], T.GE[:, 0:128:16], ["GE", "FM", "MK"], ["F2"], scale=T.MK[:, 3:4])
        act(T.FM[:, 144 + 15:144 + 143:16], T.GE[:, 0:128:16], ["GE", "FM"], ["F1"], scale=2048.0)
        nz()
        for j in range(16):
            act(l64(T.KK, j), T.X[:], ["X"], ["KK"], scale=0.0, bias=float(256 * (7 - j % 8) + 4096 + 1024 * (j // 8)))
        for j in range(8):
            act(DM(j), I1, ["I1", "AVa"], ["DM"], scale=T.AV[:, j:j + 1])
        for l in range(4):
            act(l64(T.ZS, l), T.X[:], ["X"], ["ZS"], bias=float((4 - l) * 8192 + WA - Z1 + V * l))
            act(l64(T.ZS, 4 + l), T.X[:], ["X"], ["ZS"], scale=-1.0, bias=float((4 - l) * 8192 + 4096 - V * l))
            act(T.FM[:, (3 + l) * 144 + 15:(3 + l) * 144 + 143:16], T.GE[:, 0:128:16], ["GE", "FM", "AVe"], ["F3"],
                scale=T.AV[:, 8 + l:9 + l])
        act(Ih, I1, ["I1"], ["Ih"], scale=0.5)
        act(Ihn, I1, ["I1"], ["Ihn"], scale=-0.5)

    def late_constants():
        cp(T.MI[:], T.ME[:, 0:64], ["ME"], ["MI"])
        cp(T.t2[:], T.N[:], ["N"], ["t2"])
        ts(T.MJ[:, 0:64], T.MI[:], 255, A.bitwise_and, ["MI"], ["MJ"])
        ts(T.MJ[:, 64:128], T.MI[:], 8, A.arith_shift_right, ["MI"], ["MJ2"])
        ts(T.HL[:, :, 0:64], T.t2[:], 255, A.bitwise_and, ["t2"], ["HL0"])
        ts(T.HL[:, :, 64:128], T.t2[:], 8, A.arith_shift_right, ["t2"], ["HL1"])
        ts(T.MC[:, 0:64], T.MJ[:, 0:64], 1024.0, A.add, ["MJ"], ["MC0"])
        ts(T.MC[:, 64:128], T.MJ[:, 64:128], 8.0, A.add, ["MJ2"], ["MC1"])

    pairs = [(0, 192, 64), (192, 128, 128), (320, 64, 192)]
    ek = ["EE64", "EE128", "EE192"]

    def twins_a(a, b):
        wk0 = ["w0b%d" % l for l in range(4)] + ["w0i%d" % l for l in range(4)]
        mm([(P[3][:, 0:256], I1, T.KK[:, 0:256], True, False)][a:] +
           [(P[3][:, 0:256], FM(1, i), T.W[:, WA + i:WA + 4096:16], False, i == 15) for i in range(a, b)],
           wk0 + ["KK", "I1", "F1"], ["K0"], [3])

    def twins_b():
        for (o, n, d) in pairs:
            tt(P[2][:, o:o + n], P[1][:, 256:256 + n], T.N[:, d:256], A.is_equal, ["N", "NP"], ["EE%d" % d], [1, 2])
        for (o, n, d) in pairs:
            tt(T.GT[:, o:o + n], P[3][:, 0:n], T.KS[:, d:256], A.is_gt, ["KS", "K0"], ["GT%d" % d], [3])
        tt(T.EG[:], P[2][:, 0:384], T.GT[:], A.mult, ek + ["GT64", "GT128", "GT192"], ["EG"], [2])
        tt(T.GT[:], P[2][:, 0:384], T.EG[:], A.subtract, ek + ["EG"], ["GT"], [2])

    def twins_c():
        lst = [(P[3][:, 256:512], I1, T.EMP[:], True, False)]
        for (o, n, d) in pairs:
            lst.append((P[3][:, 256 + d:512], I1, T.EG[:, o:o + n], False, False))
            lst.append((P[3][:, 256:256 + n], I1, T.GT[:, o:o + n], False, d == 192))
        mm(lst, ["EG", "GT", "EMP"], ["DUPP"], [3])
        act(T.DUP[:], P[3][:, 256:512], ["DUPP"], ["DUP"], [3], F.Sign)

    def cell(c):
        return (T.SC[:, c[1] * 128:(c[1] + 1) * 128] if c[0] == "s" else P[c[0]][:, c[1] * 128:(c[1] + 1) * 128])

    def ckey(c):
        return "c%s_%d" % c

    def cop(o, a, b, alu, oap=None, okey=None):
        bk = [c[0] for c in (o, a, b) if c is not None and c[0] != "s"]
        tt(cell(o) if oap is None else oap, cell(a), cell(b), alu, [ckey(a), ckey(b)], [okey or ckey(o)], bk)

    def ce(a, b, hi, lo):
        cop(hi, a, b, A.max)
        cop(lo, a, b, A.min)

    def sort4(c, pa, pb, pc, sa, sb_, sc_, fin):
        ce(c[0], c[1], pa, sa)
        ce(c[2], c[3], sb_, pb)
        ce(pa, sb_, fin[0], sc_)
        ce(sa, pb, pc, fin[3])
        ce(pc, sc_, fin[1], fin[2])

    CH = [(0, 16, 0, 0), (16, 32, 1024, 2), (48, 16, 3072, 1)]
    later = [None]

    for r in range(RO):
        par = r % 2
        h0, h1, t0 = r * PW, (r + 1) * PW, r * PW
        o0, o1 = par * V, (1 - par) * V
        w0 = WA if par == 0 else WB_
        hk = ["h%db" % r, "h%di" % r, "h%dj" % r, "pad", "hR%d" % r]
        ok = ["o%d" % par, "o%da" % par, "o%db" % par]
        lastw["hR%d" % r] = ("aH%d" % r, 24)
        wk = ["w%db%d" % (par, l) for l in range(4)] + ["w%di%d" % (par, l) for l in range(4)]
        Hw = T.H[:, h0:h0 + PW]

        def cmp_(k, l):
            c0, n, o, b = CH[k]
            tt(T.CMP[:, o + 16 * n * l:o + 16 * n * (l + 1)], Hw.indirect(T.N16[:, 64 * l + c0:64 * l + c0 + n]),
               T.HO[:, o0 + 16 * c0:o0 + 16 * (c0 + n)], A.is_lt, hk + ["N16", ok[k]], ["c%d%d" % (k, l)])

        def diff_s(j):
            for l in (2 * j, 2 * j + 1):
                act(T.WD[:, B * l:B * (l + 1)], Hw.indirect(T.N16[:, 64 * l + 48:64 * l + 64]), hk + ["N16"], ["WX%d" % l])
            b = P[5 + j]
            mm([(b[:, 0:512], In, T.WD[:, 512 * j:512 * (j + 1)], True, False),
                (b[:, 0:B], I1, T.HO[:, o0 + 768:o0 + V], False, False), (b[:, B:512], I1, T.HO[:, o0 + 768:o0 + V], False, True)],
               ["WX%d" % (2 * j), "WX%d" % (2 * j + 1), ok[2], "In"], ["df%d" % j], [5 + j])

        def sign_s(j):
            act(T.CMP[:, 3072 + 512 * j:3072 + 512 * (j + 1)], P[5 + j][:, 0:512], ["df%d" % j], ["c2%d" % (2 * j), "c2%d" % (2 * j + 1)],
                [5 + j], F.Sign, 1.0, -0.5)

        def votes(k, la=0, lb=4):
            c0, n, o, b = CH[k]
            ls = range(la, lb)
            lst = [(P[b][:, n * la:n * lb], FM(0, i), T.CMP[:, o + 16 * n * la + i:o + 16 * n * lb:16], i == 0, False) for i in range(16)]
            if la == 0:
                lst.append((P[b][:, 0:n], Ibig, T.DEAD[:, c0:c0 + n], False, False))
            if k == 2:
                lst.append((P[b][:, 0:64], I16, T.HALF[:], False, False))
                lst += [(P[b][:, n * l:n * l + n], I16, T.EMP[:, 64 * l + c0:64 * l + c0 + n], False, False) for l in ls]
            lst += [(P[b][:, n * l:n * l + n], I16, T.EMP[:, 64 * l + c0:64 * l + c0 + n], False, l == lb - 1) for l in ls]
            mm(lst, ["c%d%d" % (k, l) for l in ls] + ["EMP", "DEAD", "F0", "I16", "Ibig", "HALF"], ["v%d" % k], [b])

        def would(k, o, key):
            c0, n, _, b = CH[k]
            ts(T.FL[:, 4 * c0:4 * c0 + 4 * n], P[b][:, 0:4 * n], 8.5, A.is_ge, ["v%d" % k], ["FL%d" % k], [b])
            tt(T.FM2[:, 2 * c0:2 * c0 + 2 * n], T.FL[:, 4 * c0:4 * c0 + 2 * n], T.FL[:, 4 * c0 + 2 * n:4 * c0 + 4 * n], A.mult,
               ["FL%d" % k], ["F2%d" % k])
            tt(o, T.FM2[:, 2 * c0:2 * c0 + n], T.FM2[:, 2 * c0 + n:2 * c0 + 2 * n], A.mult, ["F2%d" % k], [key])

        def spread(k):
            c0, n = CH[k][0:2]
            mm([(P[4 + k][:, i:16 * n:16], XM(i), T.DIE[:, c0:c0 + n], True, True) for i in range(16)], ["DIE%d" % k, "XM"],
               ["ti%d" % k], [4 + k])

        def table(k, col):
            c0, n = CH[k][0:2]
            tt(T.TT[:, t0 + col:t0 + col + 16 * n], P[4 + k][:, 0:16 * n], T.TS[:, 16 * c0:16 * (c0 + n)], A.add, ["ti%d" % k, "TS"],
               ["t%d%d" % (r, k)], [4 + k])

        for l in range(4):
            cmp_(0, l)
        diff_s(0)
        votes(0)
        diff_s(1)
        sign_s(0)
        if r:
            later[0](0)
        sign_s(1)
        cmp_(1, 0)
        would(0, T.EB[:], "EB")
        op("v", lambda: g.vector.tensor_tensor_scan(T.ES[:], T.EB[:], T.ZERO[:], 0.0, A.add, A.add), ["EB", "ZERO"], ["ES"])
        mm([(P[3][:, 0:16], T.GE[:], T.ES[:], True, False), (P[3][:, 0:16], T.UN[:], T.EB[:], False, True)],
           ["ES", "EB", "UN", "GE"], ["pf"], [3])
        ts(T.DIE[:, 0:16], P[3][:, 0:16], -63.5, A.is_le, ["pf"], ["DIE0"], [3])
        spread(0)
        if r == 0:
            late_scalar()
        else:
            for l in range(1, 4):
                later[0](l)
        cmp_(1, 1)
        table(0, cb)
        small(T.TT[:, t0 + cb:t0 + cb + B], T.TT[:, t0 + cb:t0 + cb + B], ["t%d0" % r], "aT%d" % r, "sT%d" % r)
        votes(2)
        votes(1, 0, 2)
        if r == 0:
            twins_a(0, 8)
        cmp_(1, 2)
        cmp_(1, 3)
        votes(1, 2, 4)
        would(2, T.DIE[:, 48:64], "DIE2")
        spread(2)
        if r == 0:
            late_constants()
        would(1, T.DIE[:, 16:48], "DIE1")
        spread(1)
        table(2, ci + 512)
        tt(T.DEAD[:], T.DEAD[:], T.DIE[:], A.add, ["DEAD", "DIE0", "DIE1", "DIE2"], ["DEAD"])
        if r == 0:
            twins_a(8, 16)
        table(1, ci)

        lastw["tR%d" % r] = ("aT%d" % r, 24)
        tk = ["t%d0" % r, "t%d1" % r, "t%d2" % r, "tR%d" % r, "pad", "N16"]
        Tw = T.TT[:, t0:t0 + PW]

        def gth(e, l, a, b, key):
            gather(e, T.G[:, V * l + 16 * a:V * l + 16 * b], Tw.indirect(T.N16[:, 64 * l + a:64 * l + b]), tk, [key])

        def gone(l):
            mm([(l64(P[0], l, 256), FM(2, i), T.G[:, V * l + i:V * (l + 1):16], i == 0, False) for i in range(16)] +
               [(l64(P[0], l, 256), Ibig, T.DEAD[:], False, True)], ["gb%d" % l, "gi%d" % l, "gj%d" % l, "F2", "DEAD"], ["gn%d" % l], [0])

        def tab(l, n):
            mm([(P[4][:, 0:512], DM(l), T.G[:, V * l + B:V * l + 768], n == 0, n == 3),
                (P[5][:, 0:B], DM(l), T.G[:, V * l + 768:V * (l + 1)], n == 0, n == 3)], ["gi%d" % l, "gj%d" % l], ["mt"], [4, 5])
        for l in (0, 2, 1, 3):
            gth("v" if l < 2 else "s", l, 0, 16, "gb%d" % l)
        gb = ["gb0", "gb1", "gb2", "gb3", "DM"]
        mm([(P[7][:, 0:B], DM(4 + l), T.G[:, V * l:V * l + B], l == 0, l == 3) for l in range(4)], gb, ["mx"], [7])
        mm([(P[6][:, 0:B], DM(l), T.G[:, V * l:V * l + B], l == 0, l == 3) for l in range(4)], gb, ["mb"], [6])
        gth("v", 0, 16, 64, "gi0")
        gth("s", 2, 16, 32, "gj2")
        act(T.MX[:, r * B:(r + 1) * B], P[7][:, 0:B], ["mx"], ["MX%d" % r], [7])
        small(T.MX[:, r * B:(r + 1) * B], T.M[:, t0 + cb:t0 + cb + B], ["MX%d" % r], "aM%d" % r, "sM%d" % r)
        if r == 0:
            act(T.KS[:], P[3][:, 0:256], ["K0"], ["KS"], [3])
        gth("s", 2, 32, 64, "gi2")
        gth("v", 1, 16, 64, "gi1")
        gth("s", 3, 16, 58, "gi3")
        gth("v", 3, 58, 64, "gj3")
        if r == 0:
            twins_b()
        else:
            nz()
        gone(0)
        tab(0, 0)
        act(T.M[:, t0 + cb:t0 + cb + B], P[6][:, 0:B], ["mb"], ["m0"], [6])
        gone(2)
        gone(1)
        gone(3)
        tab(2, 1)
        tab(1, 2)
        tab(3, 3)
        gk = ["gn0", "gn1", "gn2", "gn3"]
        zs = 256 * par
        tt(T.ZA[:, 0:128], P[0][:, 256:384], T.NZ[:, 0:128], A.mult, gk + ["NZ"], ["ZA0"], [0])
        tt(P[0][:, 0:128], P[0][:, 384:512], T.NZ[:, 128:256], A.mult, gk + ["NZ"], ["ZA1"], [0])
        tt(T.ZA[:, 128:256], P[0][:, 256:384], T.ZS[:, zs:zs + 128], A.mult, gk + ["ZS"], ["ZA2"], [0])
        tt(P[0][:, 128:256], P[0][:, 384:512], T.ZS[:, zs + 128:zs + 256], A.mult, gk + ["ZS"], ["ZA3"], [0])
        for k in range(2):
            tt(l64(T.ZB, k), l64(P[0], 2 * k), l64(T.ZA, 2 * k), A.max, ["ZA%d" % (2 * k), "ZA%d" % (2 * k + 1)], ["ZB%d" % k], [0])
            tt(l64(P[6], k), l64(P[0], 2 * k + 1), l64(T.ZA, 2 * k + 1), A.max, ["ZA%d" % (2 * k), "ZA%d" % (2 * k + 1)],
               ["ZP%d" % k], [0, 6])
        act(T.M[:, t0 + ci:t0 + ci + 512], P[4][:, 0:512], ["mt"], ["m1"], [4])
        act(T.M[:, t0 + ci + 512:t0 + ci + 768], P[5][:, 0:B], ["mt"], ["m2"], [5])
        tt(T.ZC[:], P[6][:, 0:128], T.ZB[:], A.max, ["ZB0", "ZB1", "ZP0", "ZP1"], ["ZC"], [6])
        ts(T.ZI[:], T.ZC[:], 0.0, A.max, ["ZC"], ["ZI"])
        ts(T.ZD[:, 0:64], T.ZI[:, 0:64], 2047, A.bitwise_and, ["ZI"], ["ZD0"])
        ts(T.ZD[:, 64:128], T.ZI[:, 64:128], 8191, A.bitwise_and, ["ZI"], ["ZD1"])
        cp(T.OD[:], T.ZD[:, 0:64], ["ZD0"], ["OD"])
        if par == 0:
            cp(T.OS[:], T.ZD[:, 64:128], ["ZD1"], ["OS"])
        else:
            ts(T.OS[:], T.ZD[:, 64:128], -1.0, A.mult, ["ZD1"], ["OS"], (), 4096.0, A.add)
        ts(P[6][:, 128:192], T.ZD[:, 0:64], float(ci), A.is_ge, ["ZD0"], ["FD"], [6], 3392.0 if par == 0 else -4928.0, A.mult)
        ts(T.HIT[:], T.ZI[:, 0:64], 0.5, A.is_gt, ["ZI"], ["HIT"])
        tt(T.FE[:], P[6][:, 128:192], T.ZD[:, 0:64], A.add, ["FD", "ZD0"], ["FE"], [6])
        for l in range(4):
            ts(l64(T.OW, l), T.FE[:], float(V * l + (-16 if par == 0 else 4144)), A.add, ["FE"], ["OW%d" % l])

        lastw["mR%d" % r] = ("aM%d" % r, 24)
        act(T.MD[:], T.M[:, t0:t0 + PW].indirect(T.OD[:]), ["m0", "m1", "m2", "mR%d" % r, "OD", "pad"], ["MD"])
        if r == 0:
            twins_c()
        act(T.GS[:], P[0][:, 256:512], gk, ["GS"], [0], F.Relu)
        KO = P[1][:, 0:256]
        mm([(KO, I1, T.KK[:, 512 * par:512 * par + 256], True, False)] +
           [(KO, FM(1, i), T.W[:, w0 + i:w0 + 4096:16], False, False) for i in range(KOA)] +
           [(KO, Ibig, T.EMP[:], False, False)], wk + ["KK", "F1", "EMP"], ["KO"], [1])
        sw = T.W[:, Z1:CW] if par == 0 else T.W[:, WB_:RB]
        cp(T.WS[:], sw.indirect(T.OS[:]), wk + ["OS", "pad"], ["WS"])
        for l in range(4):
            mm([(l64(P[2], l), FM(3 + l, i), T.MD[:, i:V:16], i == 0, i == 15) for i in range(16)], ["MD", "F3"], ["nc%d" % l], [2])
        mm([(KO, FM(1, i), T.W[:, w0 + i:w0 + 4096:16], False, False) for i in range(KOA, 16)] +
           [(KO, Ibig, T.DUP[:], False, False), (KO, Ibig, T.GS[:], False, True)], wk + ["GS", "DUP"], ["KO"], [1])
        lastw["rR%d" % r] = ("aW%d" % r, 16)
        lastw["rS%d" % r] = ("st%d" % r, 8)
        dw = T.W[:, RA:CW] if par == 0 else T.W[:, WB_:WEND]
        dk = wk + ["r%do%d" % (par, l) for l in range(4)] + ["rR%d" % r, "rS%d" % r, "pad"]
        tt(T.TN[:], Hw.indirect(T.OD[:]), T.WS[:], A.subtract, hk + ["OD", "WS"], ["TN"])
        nk = ["nc0", "nc1", "nc2", "nc3"]
        NC = P[2][:, 0:256]

        def wd(l):
            act(T.WD[:, V * l:V * (l + 1)], dw.indirect(l64(T.OW, l)), dk + ["OW%d" % l],
                ["WD%d" % l] + (["WX0", "WX1", "WX2", "WX3"] if l == 0 else []))

        def wd_add(l):
            for k in range(2):
                b = 4 + 2 * (l % 2) + k
                mm([(P[b][:, 0:512], I1, T.WD[:, V * l + 512 * k:V * l + 512 * (k + 1)], True, False),
                    (P[b][:, 0:512], In, T.TN[:, 512 * k:512 * (k + 1)], False, True)], ["WD%d" % l, "TN", "In"], ["x%d" % b], [b])

        def clip(l, k, e):
            b = 4 + 2 * (l % 2) + k
            o = T.W[:, CW + V * l + 512 * k:CW + V * l + 512 * (k + 1)]
            if e == "v":
                ts(o, P[b][:, 0:512], 0.0, A.max, ["x%d" % b], ["cw%d%d" % (l, k)], [b], 255.0, A.min)
            else:
                q = 2 * l + k - 5
                act(T.CL[:, 512 * q:512 * (q + 1)], P[b][:, 0:512], ["x%d" % b], ["CL%d" % q], [b], F.Relu, -1.0, 255.0)
                act(o, T.CL[:, 512 * q:512 * (q + 1)], ["CL%d" % q], ["cw%d%d" % (l, k)], (), F.Relu, -1.0, 255.0)

        def sums(l, last):
            mm([(l64(P[3], l), FM(1, i), T.W[:, CW + V * l + i:CW + V * (l + 1):16], False, last and i == 15) for i in range(16)],
               ["cw%d0" % l, "cw%d1" % l], ["KC"], [3])
        wd(0)
        for l in range(4):
            act(l64(T.FO, l), T.HIT[:], ["HIT"], ["FO"], scale=-2 * BIG, bias=float(2 ** 23 + 256 * (7 - l) + 1024 * par))
        wd(1)
        wd_add(0)
        cp(T.NCI[:], NC, nk, ["NCI"], [2])
        tt(T.EM[:], NC, T.ME[:], A.is_equal, nk + ["ME"], ["EM"], [2])
        for d in range(4):
            n = 256 - 64 * d
            tt(T.E[:, 256 * d:256 * d + n], P[2][:, 0:n], T.N[:, 64 * d:256], A.is_equal, nk + ["N"], ["E%d" % d], [2])
            if d:
                tt(T.E[:, 256 * d + n:256 * (d + 1)], P[2][:, n:256], T.N[:, 0:64 * d], A.is_equal, nk + ["N"], ["Eb%d" % d], [2])
        for (o, n, d) in pairs:
            tt(T.EE[:, o:o + n], P[2][:, 0:n], T.NCI[:, d:256], A.is_equal, nk + ["NCI"], ["EE%d" % d], [2])
        wd_add(1)
        clip(0, 0, "v")
        clip(0, 1, "v")
        wd(2)
        mm([(P[3][:, 0:256], I1, T.KK[:, 512 * par + 256:512 * par + 512], True, False),
            (P[3][:, 0:256], Ibig, T.EM[:], False, False)], ["EM"], ["KC"], [3])
        lst = [(P[2][:, 256:512], Ibig, T.E[:, 0:256], True, False)]
        for d in range(1, 4):
            n = 256 - 64 * d
            lst.append((P[2][:, 256 + 64 * d:512], Ibig, T.E[:, 256 * d:256 * d + n], False, False))
            lst.append((P[2][:, 256:256 + 64 * d], Ibig, T.E[:, 256 * d + n:256 * (d + 1)], False, d == 3))
        mm(lst, ["E0", "E1", "E2", "E3", "Eb1", "Eb2", "Eb3"], ["KILL"], [2])
        mm([(P[0][:, 256 + d:512], I1, T.EE[:, o:o + n], d == 64, d == 192) for (o, n, d) in pairs], ek, ["al"], [0])
        sums(0, False)
        act(T.PEN[:], NC, nk, ["PEN"], [2], F.Relu, -1.0)
        wd(3)
        clip(1, 0, "v")
        clip(1, 1, "v")
        wd_add(2)
        mm([(P[3][:, 0:256], Ibig, T.PEN[:], False, False)], ["PEN"], ["KC"], [3])
        sums(1, False)
        wd_add(3)
        clip(2, 1, "s")
        clip(3, 0, "s")
        clip(3, 1, "s")
        tt(T.U[:], KO, T.E[:, 0:256], A.mult, ["KO", "E0"], ["U"], [1])
        tt(T.T2[:], KO, T.FO[:], A.max, ["KO", "FO"], ["T2"], [1])
        for d in range(1, 4):
            n = 256 - 64 * d
            o = 0 if d == 2 else 256
            bb = 0 if d == 2 else 1
            tt(P[bb][:, o:o + n], P[1][:, 64 * d:256], T.E[:, 256 * d:256 * d + n], A.mult, ["KO", "E%d" % d, "N", "NZ"], ["pa%d" % d], [1, bb])
            tt(P[bb][:, o + n:o + 256], P[1][:, 0:64 * d], T.E[:, 256 * d + n:256 * (d + 1)], A.mult, ["KO", "Eb%d" % d],
               ["pb%d" % d], [1, bb])
            if d == 1:
                ts(T.AL[:], P[0][:, 320:512], 0.5, A.is_lt, ["al"], ["AL"], [0])
            elif d == 2:
                ts(T.LOC[:], T.NCI[:], 255, A.bitwise_and, ["NCI"], ["LOC"])
            else:
                ts(T.HIC[:], T.NCI[:], 8, A.arith_shift_right, ["NCI"], ["HIC"], (), 7, A.bitwise_and)
            tt(T.U[:], P[bb][:, o:o + 256], T.U[:], A.max, ["U", "pa%d" % d, "pb%d" % d], ["U"], [bb])
        tt(P[1][:, 256:512], P[2][:, 256:512], T.T2[:], A.add, ["KILL", "T2", "U"], ["T3"], [1, 2])
        clip(2, 0, "v")
        sums(2, False)
        sums(3, True)
        for a in range(4):
            for k in range(2):
                tt(P[0][:, 128 * a + 64 * k:128 * a + 64 * k + 64], l64(P[1], a, 256), T.HL[:, a, 64 * k:64 * k + 64],
                   A.add, ["T3", "HL%d" % k, "U"], ["k%d%d" % (a, k)], [0, 1])
        c0 = [(0, 0), ("s", 0), (0, 2), ("s", 1)]
        for a in range(4):
            tt(cell(c0[a]), P[0][:, 128 * a:128 * a + 128], T.MC[:], A.max, ["k%d0" % a, "k%d1" % a, "MC0", "MC1"], [ckey(c0[a])], [0])
        own4 = [("s", 5), ("s", 6), ("s", 7), ("s", 8)]
        sort4(c0, (0, 1), (0, 3), (0, 0), ("s", 2), ("s", 3), ("s", 4), own4)

        def height(k, a, n, hc, b1, b2, key):
            ho = T.HO[:, o0 + a:o0 + a + n]
            mm([(P[b1][:, 0:n], Ih, T.WS[:, a:a + n], True, False), (P[b1][:, 0:n], Ihn, ho, False, True)],
               ["WS", ok[k], "Ih", "Ihn"], ["hd"], [b1])
            act(T.HU[:, a:a + n], P[b1][:, 0:n], ["hd"], ["HU%d" % a], [b1], bias=127.8)
            act(T.HF[:, a:a + n], T.HU[:, a:a + n], ["HU%d" % a], ["HF%d" % a], (), F.Relu, 1.0, -128.0)
            mm([(P[b2][:, 0:n], I1, T.HF[:, a:a + n], True, False), (P[b2][:, 0:n], I1, ho, False, True)],
               ["HF%d" % a, ok[k]], ["he"], [b2])
            if r + 1 < RO:
                act(T.H[:, h1 + hc:h1 + hc + n], P[b2][:, 0:n], ["he"], [key], [b2])
            act(T.HO[:, o1 + a:o1 + a + n], P[b2][:, 0:n], ["he"], [("o%d" % (1 - par)) + ("", "a", "b")[k]], [b2])
        height(0, 0, B, cb, 4, 5, "h%db" % (r + 1))
        if r + 1 < RO:
            small(T.H[:, h1 + cb:h1 + cb + B], T.H[:, h1 + cb:h1 + cb + B], ["h%db" % (r + 1)], "aH%d" % (r + 1), "sH%d" % (r + 1))
        for l in range(4):
            act(l64(P[2], l, 256), T.X[:], ["X", "T3"], ["XS"], [2], scale=-0.25 if par else 0.25, bias=272.0 if par else 1808.0)
        height(1, B, 512, ci, 4, 5, "h%di" % (r + 1))
        height(2, 768, B, ci + 512, 7, 4, "h%dj" % (r + 1))
        if r + 1 == RO:
            dma("y", T.yh[:], T.HO[:, o1:o1 + V], ["o1", "o1a", "o1b"], [], "out")
        else:
            mm([(P[7][:, 0:256], I1, T.DUP[:], True, False)] +
               [(l64(P[7], l), In, T.HIT[:], False, l == 3) for l in range(4)], ["DUP", "HIT"], ["dp"], [7])
            act(T.DUP[:], P[7][:, 0:256], ["dp"], ["DUP"], [7], F.Relu)

        Y = P[1]
        tt(Y[:, 256:512], P[3][:, 0:256], T.U[:], A.max, ["KC", "U"], ["Y"], [1, 3])
        for (o, n, d) in pairs:
            tt(T.XX[:, o:o + n], Y[:, 256 + d:512], T.EE[:, o:o + n], A.mult, ["Y", "EE%d" % d], ["XX%d" % d], [1])
        for (o, n, d) in pairs:
            tt(Y[:, 256:256 + n], Y[:, 256:256 + n], T.XX[:, o:o + n], A.max, ["Y", "XX64", "XX128", "XX192"], ["Y"], [1])
        tt(P[2][:, 64:256], Y[:, 320:512], T.AL[:], A.mult, ["Y", "AL"], ["D"], [1, 2])
        for a in range(4):
            for k in range(2):
                t = T.SC if c0[a][0] == "s" else P[0]
                o = 128 * c0[a][1] + 64 * k
                tt(t[:, o:o + 64], l64(P[2], a) if a else Y[:, 256:320], l64(T.HIC if k else T.LOC, a), A.add,
                   ["D" if a else "Y", "LOC", "HIC"], [ckey(c0[a])], [0, 1, 2])
        b4 = [(6, 0), (6, 1), (6, 2), (6, 3)]
        sort4(c0, (0, 1), (0, 3), (0, 0), ("s", 2), ("s", 3), ("s", 4), b4)
        m = [(0, 1), (0, 2), ("s", 9), ("s", 10)]
        for j in (0, 3, 1, 2):
            cop(m[j], own4[j], b4[3 - j], A.max)
        ce(m[0], m[2], (6, 0), (6, 1))
        ce(m[1], m[3], ("s", 11), ("s", 12))
        for j, (a, b) in enumerate((((6, 0), ("s", 11)), ((6, 1), ("s", 12)))):
            cop(None, a, b, A.max, T.RI[:, 2 * j, :], "RI%d" % (2 * j))
            cop(None, a, b, A.min, T.RI[:, 2 * j + 1, :], "RI%d" % (2 * j + 1))
        rk = ["RI0", "RI1", "RI2", "RI3"]
        R1, R2 = T.RI[:, :, 0:64], T.RI[:, :, 64:128]

        def names():
            ts(T.HL[:, :, 64:128], R2, 7, A.bitwise_and, rk, ["HL1"])
            ts(T.HL[:, :, 0:64], R1, 255, A.bitwise_and, rk, ["HL0"])
            ts(P[1][:, 0:256], T.HL[:, :, 64:128], 256.0, A.mult, ["HL1"], ["nh"], [1])
            tt(NP, P[1][:, 0:256], T.HL[:, :, 0:64], A.add, ["nh", "HL0"], ["NP"], [1])

        ts(T.da[:], R2, 1792, A.bitwise_and, rk, ["da"])
        tt(P[2][:, 0:256], P[2][:, 256:512], T.da[:], A.add if par else A.subtract, ["da", "XS"], ["dc"], [2])
        tt(T.db[:], P[2][:, 0:256], R2, A.min, ["dc"] + rk, ["db"], [2])
        ts(T.OM[:], T.db[:], -4.0 if par else 4.0, A.mult, ["db"], ["OM"], (), 8256.0 if par else 0.0, A.add)
        mw = T.W[:, Z1:WB_] if par == 0 else T.W[:, CW:RB]
        mk = wk + ["cw%d%d" % (l, k) for l in range(4) for k in range(2)] + ["pad", "OM"]
        if r + 1 < RO:
            wn = WB_ if par == 0 else WA
            kn = "w%d" % (1 - par)
            names()
            cp(T.N16[:], NP, ["NP"], ["N16"], [1])
            tt(T.EMP[:], NP, T.ME[:], A.is_equal, ["NP", "ME"], ["EMP"], [1])
            for l in range(4):
                act(T.W[:, wn + V * l:wn + V * l + B], mw.indirect(T.OM[:, 64 * l:64 * l + 16]), mk, [kn + "b%d" % l])
            wsend(r + 1)
            later[0] = lambda l, wn=wn, mw=mw, mk=mk, kn=kn: act(
                T.W[:, wn + V * l + B:wn + V * (l + 1)], mw.indirect(T.OM[:, 64 * l + 16:64 * l + 64]), mk, [kn + "i%d" % l])
        else:
            def piece(e, a, b):
                gather(e, T.YW[:, 16 * a:16 * b], mw.indirect(T.OM[:, a:b]), mk, ["y%d" % a])
                dma("y", T.yw[:, 16 * a:16 * b], T.YW[:, 16 * a:16 * b], ["y%d" % a], [], "out")
            piece("s", 0, 48)
            names()
            ts(T.t1[:], NP, -16.0, A.add, ["NP"], ["t1"], [1])
            piece("s", 48, 96)
            ts(T.t2[:], T.t1[:], 1792, A.bitwise_and, ["t1"], ["t2"])
            ts(T.de[:], T.t1[:], 1023.5, A.is_gt, ["t1"], ["de"], (), float(V * rank - 768 - 3072), A.mult)
            ts(P[2][:, 0:256], T.t2[:], 1024.0, A.min, ["t2"], ["e1"], [2], 3.0, A.mult)
            tt(P[2][:, 256:512], P[2][:, 0:256], T.t1[:], A.add, ["e1", "t1"], ["e2"], [2])
            tt(T.YN[:], P[2][:, 256:512], T.de[:], A.add, ["e2", "de"], ["YN"], [2])
            dma("y", T.yn[:], T.YN[:], ["YN"], [], "out")
            for e, a, b in (("s", 96, 144), ("v", 178, 224), ("s", 144, 178), ("v", 224, 256)):
                piece(e, a, b)
    for k in sorted(cnt):
        if k in ("cv", "cs", "cp"):
            wait("y", (k, cnt[k]))
        elif k != "out":
            wait("g", (k, cnt[k]))
    wait("y", ("out", cnt["out"]))
